import numpy as np
import ml_dtypes


def mxq(x, axis, fmt="e4m3"):
    dtype, down = {"e4m3": (ml_dtypes.float8_e4m3fn, 7), "e5m2": (ml_dtypes.float8_e5m2, 14)}[fmt]
    v = np.moveaxis(np.asarray(x, np.float32).astype(ml_dtypes.bfloat16).astype(np.float64), axis, -1)
    blocks = v.reshape(v.shape[:-1] + (-1, 32))
    amax = np.abs(blocks).max(-1, keepdims=True)
    byte = np.maximum(np.where(amax > 0, np.frexp(amax)[1] - 1 + 127, 0) - down, 1)
    scale = np.exp2(byte - 127.0)
    codes = (blocks / scale).astype(np.float32).astype(dtype).astype(np.float64)
    return np.moveaxis((codes * scale).reshape(v.shape), -1, axis)


WIDE = False


def mx_kscale(k):
    if not WIDE:
        return np.ones(k)
    levels = np.array([30, -30])
    if k % 512:
        return np.exp2(np.random.permutation(np.resize(levels, k // 32))).repeat(32)
    a = np.empty((k // 512, 16))
    for p in range(k // 512):
        a[p, :8] = np.random.permutation(np.resize(levels, 8))
        for g in range(8):
            far = levels[np.abs(levels - a[p, g]) >= 10]
            a[p, g + 8] = far[np.random.randint(len(far))]
    return np.exp2(a.ravel()).repeat(32)


def f64(x):
    return np.asarray(x).astype(np.float64)


K, L, M, N = 2048, 512, 256, 1536


def setup_inputs():
    n = np.random.standard_normal
    s1 = mx_kscale(K)[:, None]
    s2 = mx_kscale(L)[:, None]
    m1, m2 = np.exp(0.5 * n((1, M))), np.exp(0.5 * n((1, N)))
    return {
        "x": (n((K, M)) / np.sqrt(K) * s1).astype(np.float32),
        "xt": (n((K, N)) / s1).astype(np.float32),
        "g": (m1 * n((L, M)) / np.sqrt(L) * s2).astype(np.float32),
        "gt": (m2 * n((L, N)) / s2).astype(np.float32),
    }


def reference(x, xt, g, gt):
    x_ = mxq(f64(x), 0, "e4m3")
    xt_ = mxq(f64(xt), 0, "e4m3")
    g_ = mxq(f64(g), 0, "e5m2")
    gt_ = mxq(f64(gt), 0, "e5m2")
    y = x_.T @ xt_
    u = g_.T @ gt_
    y = y * u
    return y

@@ -1,0 +1,188 @@
+from contextlib import ExitStack
+from functools import partial
+
+import concourse.mybir as mybir
+
+K, L, M, N = 2048, 512, 256, 1536
+FLOPS = 2 * M * N * (K + L)
+
+F32 = mybir.dt.float32
+BF16 = mybir.dt.bfloat16
+U32 = mybir.dt.uint32
+U8 = mybir.dt.uint8
+E4M3X4 = mybir.dt.float8_e4m3fn_x4
+E5M2X4 = mybir.dt.float8_e5m2_x4
+MULT = mybir.AluOpType.mult
+
+P = 128
+PACK = 4
+K_PASS = P * PACK
+PASSES = K // K_PASS
+BLOCK = 512
+M_TILES = M // P
+
+CHUNKS = [(0, 512), (512, 512), (1024, 256), (1280, 256)]
+LAST_SHARE = [352, 152, 96, 160]
+
+
+def tile_mix_ghost_none_kernel(tc, x, xt, g, gt, out):
+    nc = tc.nc
+    with ExitStack() as ctx:
+        ctx.enter_context(tc.manual_schedule())
+        raws = ctx.enter_context(tc.tile_pool(name="raws", bufs=1))
+        keep = ctx.enter_context(tc.tile_pool(name="keep", bufs=1))
+        group_pool = ctx.enter_context(tc.tile_pool(name="groups", bufs=4))
+        psum = ctx.enter_context(tc.psum_pool(name="psum", bufs=8))
+
+        def rows(ap, c):
+            return ap[c * K_PASS : (c + 1) * K_PASS, :].rearrange("(p j) n -> p j n", j=PACK)
+
+        g_raw = raws.tile([P, PACK, M], F32, name="g_raw")
+        nc.sync.dma_start(out=g_raw[:], in_=rows(g, 0))
+        gt_raw = raws.tile([P, PACK, N], F32, name="gt_raw")
+        nc.sync.dma_start(out=gt_raw[:], in_=rows(gt, 0))
+        x_raw = raws.tile([P, PASSES, PACK, M], F32, name="x_raw")
+        nc.sync.dma_start(
+            out=x_raw[:].rearrange("p c j m -> p c (j m)"),
+            in_=x.rearrange("(c p j) m -> p c (j m)", p=P, j=PACK),
+        )
+        xt_raw = []
+        for c in range(PASSES - 1):
+            r = raws.tile([P, PACK, N], F32, name="xt_raw%d" % c)
+            nc.sync.dma_start(out=r[:], in_=rows(xt, c))
+            xt_raw.append(r)
+        last_raw = []
+        for q, (n0, w) in enumerate(CHUNKS):
+            r = raws.tile([P, PACK, w], F32, name="xt_last%d" % q)
+            nc.sync.dma_start(out=r[:], in_=rows(xt, PASSES - 1)[:, :, n0 : n0 + w])
+            last_raw.append(r)
+
+        g_codes = keep.tile([P, M], U32, align_bytes=256, name="g_codes")
+        g_scales = keep.tile([P, M], U8, align_bytes=256, name="g_scales")
+        gt_codes = keep.tile([P, N], U32, align_bytes=256, name="gt_codes")
+        gt_scales = keep.tile([P, N], U8, align_bytes=256, name="gt_scales")
+        x_codes = keep.tile([P, PASSES, M], U32, align_bytes=256, name="x_codes")
+        x_scales = keep.tile([P, PASSES, M], U8, align_bytes=256, name="x_scales")
+        xt_codes = keep.tile([P, PASSES, N], U32, align_bytes=256, name="xt_codes")
+        xt_scales = keep.tile([P, PASSES, N], U8, align_bytes=256, name="xt_scales")
+        u = keep.tile([P, M_TILES, N], F32, name="u")
+        res = [keep.tile([P, M_TILES, w], F32, name="res%d" % q) for q, (n0, w) in enumerate(CHUNKS)]
+
+        def interleave(raw, width, share):
+            grouped = group_pool.tile([P, BLOCK, PACK], BF16, align_bytes=256, name="grouped")
+            for copy, lo, hi in ((nc.vector.tensor_copy, 0, share), (nc.scalar.copy, share, width)):
+                copy(
+                    out=grouped[:, lo:hi, :].rearrange("p (c i) t -> p c t i", i=4),
+                    in_=raw[:, :, lo:hi].rearrange("p t (c i) -> p c t i", i=4),
+                )
+            return grouped
+
+        def quantize(grouped, width, codes, scales, fmt):
+            nc.vector.quantize_mx(
+                out=codes.bitcast(fmt),
+                scales=scales,
+                in_=grouped[:, :width, :].rearrange("p w j -> p (w j)"),
+            )
+
+        def run(blocks):
+            pending = None
+            for raw, width, share, codes, scales, fmt, then in blocks:
+                grouped = interleave(raw, width, share)
+                if pending is not None:
+                    pending()
+                def finish(grouped=grouped, width=width, codes=codes, scales=scales, fmt=fmt, then=then):
+                    quantize(grouped, width, codes, scales, fmt)
+                    then()
+                pending = finish
+            pending()
+
+        def nothing():
+            return None
+
+        def u_block(b):
+            cols = slice(b * BLOCK, (b + 1) * BLOCK)
+            for m in range(M_TILES):
+                mc = slice(m * P, (m + 1) * P)
+                bank = psum.tile([P, BLOCK], F32, name="bank")
+                nc.tensor.matmul_mx(
+                    out=bank[:],
+                    lhsT=g_codes[:, mc].bitcast(E5M2X4),
+                    lhsT_scale=g_scales[:, mc],
+                    rhs=gt_codes[:, cols].bitcast(E5M2X4),
+                    rhs_scale=gt_scales[:, cols],
+                    start=True,
+                    stop=True,
+                )
+                nc.scalar.copy(out=u[:, m, cols], in_=bank[:])
+
+        blocks = [(g_raw[:], M, 160, g_codes[:], g_scales[:], E5M2X4, nothing)]
+        for b in range(N // BLOCK):
+            cols = slice(b * BLOCK, (b + 1) * BLOCK)
+            blocks.append((gt_raw[:, :, cols], BLOCK, 320, gt_codes[:, cols], gt_scales[:, cols], E5M2X4, partial(u_block, b)))
+        run(blocks)
+
+        run([(x_raw[:, c], M, 160, x_codes[:, c, :], x_scales[:, c, :], E4M3X4, nothing) for c in range(PASSES)])
+
+        acc = []
+        for q in range(len(CHUNKS)):
+            acc.append([psum.tile([P, BLOCK], F32, name="bank") for m in range(M_TILES)])
+
+        def a_chunk(c, q):
+            n0, w = CHUNKS[q]
+            cols = slice(n0, n0 + w)
+            for m in range(M_TILES):
+                mc = slice(m * P, (m + 1) * P)
+                nc.tensor.matmul_mx(
+                    out=acc[q][m][:, :w],
+                    lhsT=x_codes[:, c, mc].bitcast(E4M3X4),
+                    lhsT_scale=x_scales[:, c, mc],
+                    rhs=xt_codes[:, c, cols].bitcast(E4M3X4),
+                    rhs_scale=xt_scales[:, c, cols],
+                    start=(c == 0),
+                    stop=(c == PASSES - 1),
+                )
+
+        def a_chunks(c, qs):
+            for q in qs:
+                a_chunk(c, q)
+
+        for c in range(PASSES - 1):
+            blocks = []
+            for b, qs in enumerate(((0,), (1,), (2, 3))):
+                cols = slice(b * BLOCK, (b + 1) * BLOCK)
+                blocks.append((xt_raw[c][:, :, cols], BLOCK, 320, xt_codes[:, c, cols], xt_scales[:, c, cols], E4M3X4, partial(a_chunks, c, qs)))
+            run(blocks)
+
+        last = PASSES - 1
+        grouped_of = {}
+
+        def copy(q):
+            grouped_of[q] = interleave(last_raw[q][:], CHUNKS[q][1], LAST_SHARE[q])
+
+        def quant(q):
+            n0, w = CHUNKS[q]
+            cols = slice(n0, n0 + w)
+            quantize(grouped_of[q], w, xt_codes[:, last, cols], xt_scales[:, last, cols], E4M3X4)
+            a_chunk(last, q)
+
+        def mul(q, m):
+            n0, w = CHUNKS[q]
+            nc.vector.tensor_tensor(out=res[q][:, m, :], in0=acc[q][m][:, :w], in1=u[:, m, n0 : n0 + w], op=MULT)
+            nc.sync.dma_start(out=out[m * P : (m + 1) * P, n0 : n0 + w], in_=res[q][:, m, :])
+
+        copy(0)
+        quant(0)
+        mul(0, 0)
+        mul(0, 1)
+        copy(1)
+        quant(1)
+        copy(2)
+        quant(2)
+        mul(1, 0)
+        copy(3)
+        mul(1, 1)
+        quant(3)
+        mul(2, 0)
+        mul(2, 1)
+        mul(3, 0)
+        mul(3, 1)

@@ -22,7 +22,8 @@ BLOCK = 512
 M_TILES = M // P
 
 CHUNKS = [(0, 512), (512, 512), (1024, 256), (1280, 256)]
-LAST_SHARE = [352, 152, 96, 160]
+LAST_SHARE = [256, 256, 0, 0]
+EARLY_X = 2
 
 
 def tile_mix_ghost_none_kernel(tc, x, xt, g, gt, out):
@@ -41,16 +42,14 @@ def tile_mix_ghost_none_kernel(tc, x, xt, g, gt, out):
         nc.sync.dma_start(out=g_raw[:], in_=rows(g, 0))
         gt_raw = raws.tile([P, PACK, N], F32, name="gt_raw")
         nc.sync.dma_start(out=gt_raw[:], in_=rows(gt, 0))
-        x_raw = raws.tile([P, PASSES, PACK, M], F32, name="x_raw")
-        nc.sync.dma_start(
-            out=x_raw[:].rearrange("p c j m -> p c (j m)"),
-            in_=x.rearrange("(c p j) m -> p c (j m)", p=P, j=PACK),
-        )
-        xt_raw = []
+        x_raw = [raws.tile([P, PACK, M], F32, name="x_raw%d" % c) for c in range(PASSES)]
+        xt_raw = [raws.tile([P, PACK, N], F32, name="xt_raw%d" % c) for c in range(PASSES - 1)]
+        for c in range(EARLY_X):
+            nc.sync.dma_start(out=x_raw[c][:], in_=rows(x, c))
         for c in range(PASSES - 1):
-            r = raws.tile([P, PACK, N], F32, name="xt_raw%d" % c)
-            nc.sync.dma_start(out=r[:], in_=rows(xt, c))
-            xt_raw.append(r)
+            nc.sync.dma_start(out=xt_raw[c][:], in_=rows(xt, c))
+        for c in range(EARLY_X, PASSES):
+            nc.sync.dma_start(out=x_raw[c][:], in_=rows(x, c))
         last_raw = []
         for q, (n0, w) in enumerate(CHUNKS):
             r = raws.tile([P, PACK, w], F32, name="xt_last%d" % q)
@@ -71,6 +70,8 @@ def tile_mix_ghost_none_kernel(tc, x, xt, g, gt, out):
         def interleave(raw, width, share):
             grouped = group_pool.tile([P, BLOCK, PACK], BF16, align_bytes=256, name="grouped")
             for copy, lo, hi in ((nc.vector.tensor_copy, 0, share), (nc.scalar.copy, share, width)):
+                if lo == hi:
+                    continue
                 copy(
                     out=grouped[:, lo:hi, :].rearrange("p (c i) t -> p c t i", i=4),
                     in_=raw[:, :, lo:hi].rearrange("p t (c i) -> p c t i", i=4),
@@ -118,10 +119,13 @@ def tile_mix_ghost_none_kernel(tc, x, xt, g, gt, out):
         blocks = [(g_raw[:], M, 160, g_codes[:], g_scales[:], E5M2X4, nothing)]
         for b in range(N // BLOCK):
             cols = slice(b * BLOCK, (b + 1) * BLOCK)
-            blocks.append((gt_raw[:, :, cols], BLOCK, 320, gt_codes[:, cols], gt_scales[:, cols], E5M2X4, partial(u_block, b)))
+            blocks.append((gt_raw[:, :, cols], BLOCK, 256, gt_codes[:, cols], gt_scales[:, cols], E5M2X4, partial(u_block, b)))
         run(blocks)
 
-        run([(x_raw[:, c], M, 160, x_codes[:, c, :], x_scales[:, c, :], E4M3X4, nothing) for c in range(PASSES)])
+        def x_blocks(cs):
+            return [(x_raw[c][:], M, 128, x_codes[:, c, :], x_scales[:, c, :], E4M3X4, nothing) for c in cs]
+
+        run(x_blocks(range(EARLY_X)))
 
         acc = []
         for q in range(len(CHUNKS)):
@@ -150,8 +154,12 @@ def tile_mix_ghost_none_kernel(tc, x, xt, g, gt, out):
             blocks = []
             for b, qs in enumerate(((0,), (1,), (2, 3))):
                 cols = slice(b * BLOCK, (b + 1) * BLOCK)
-                blocks.append((xt_raw[c][:, :, cols], BLOCK, 320, xt_codes[:, c, cols], xt_scales[:, c, cols], E4M3X4, partial(a_chunks, c, qs)))
+                then = partial(a_chunks, c, qs) if c < EARLY_X else nothing
+                blocks.append((xt_raw[c][:, :, cols], BLOCK, 288, xt_codes[:, c, cols], xt_scales[:, c, cols], E4M3X4, then))
             run(blocks)
+        run(x_blocks(range(EARLY_X, PASSES)))
+        for c in range(EARLY_X, PASSES - 1):
+            a_chunks(c, range(len(CHUNKS)))
 
         last = PASSES - 1
         grouped_of = {}
@@ -172,17 +180,12 @@ def tile_mix_ghost_none_kernel(tc, x, xt, g, gt, out):
 
         copy(0)
         quant(0)
-        mul(0, 0)
-        mul(0, 1)
         copy(1)
-        quant(1)
-        copy(2)
-        quant(2)
-        mul(1, 0)
-        copy(3)
-        mul(1, 1)
-        quant(3)
-        mul(2, 0)
-        mul(2, 1)
-        mul(3, 0)
-        mul(3, 1)
+        mul(0, 0)
+        for q in range(1, len(CHUNKS)):
+            quant(q)
+            if q + 1 < len(CHUNKS):
+                copy(q + 1)
+            mul(q - 1, 1)
+            mul(q, 0)
+        mul(len(CHUNKS) - 1, 1)

@@ -18,12 +18,11 @@ P = 128
 PACK = 4
 K_PASS = P * PACK
 PASSES = K // K_PASS
+LAST = PASSES - 1
 BLOCK = 512
 M_TILES = M // P
 
-CHUNKS = [(0, 512), (512, 512), (1024, 256), (1280, 256)]
-LAST_SHARE = [256, 256, 0, 0]
-EARLY_X = 2
+CHUNKS = [(0, 512, 256), (512, 512, 288), (1024, 256, 0), (1280, 256, 0)]
 
 
 def tile_mix_ghost_none_kernel(tc, x, xt, g, gt, out):
@@ -39,22 +38,24 @@ def tile_mix_ghost_none_kernel(tc, x, xt, g, gt, out):
             return ap[c * K_PASS : (c + 1) * K_PASS, :].rearrange("(p j) n -> p j n", j=PACK)
 
         g_raw = raws.tile([P, PACK, M], F32, name="g_raw")
-        nc.sync.dma_start(out=g_raw[:], in_=rows(g, 0))
         gt_raw = raws.tile([P, PACK, N], F32, name="gt_raw")
+        x_early = raws.tile([P, LAST, PACK, M], F32, name="x_early")
+        x_last = raws.tile([P, PACK, M], F32, name="x_last")
+        xt_raw = [raws.tile([P, PACK, N], F32, name="xt_raw%d" % c) for c in range(LAST)]
+        chunk_raw = [raws.tile([P, PACK, w], F32, name="chunk_raw%d" % q) for q, (n0, w, v) in enumerate(CHUNKS)]
+        x_raw = [x_early[:, c] for c in range(LAST)] + [x_last[:]]
+
+        nc.sync.dma_start(out=g_raw[:], in_=rows(g, 0))
         nc.sync.dma_start(out=gt_raw[:], in_=rows(gt, 0))
-        x_raw = [raws.tile([P, PACK, M], F32, name="x_raw%d" % c) for c in range(PASSES)]
-        xt_raw = [raws.tile([P, PACK, N], F32, name="xt_raw%d" % c) for c in range(PASSES - 1)]
-        for c in range(EARLY_X):
-            nc.sync.dma_start(out=x_raw[c][:], in_=rows(x, c))
-        for c in range(PASSES - 1):
+        nc.sync.dma_start(
+            out=x_early[:].rearrange("p c j m -> p c (j m)"),
+            in_=x[: LAST * K_PASS, :].rearrange("(c p j) m -> p c (j m)", p=P, j=PACK),
+        )
+        for c in range(LAST):
             nc.sync.dma_start(out=xt_raw[c][:], in_=rows(xt, c))
-        for c in range(EARLY_X, PASSES):
-            nc.sync.dma_start(out=x_raw[c][:], in_=rows(x, c))
-        last_raw = []
-        for q, (n0, w) in enumerate(CHUNKS):
-            r = raws.tile([P, PACK, w], F32, name="xt_last%d" % q)
-            nc.sync.dma_start(out=r[:], in_=rows(xt, PASSES - 1)[:, :, n0 : n0 + w])
-            last_raw.append(r)
+        nc.sync.dma_start(out=x_last[:], in_=rows(x, LAST))
+        for q, (n0, w, v) in enumerate(CHUNKS):
+            nc.sync.dma_start(out=chunk_raw[q][:], in_=rows(xt, LAST)[:, :, n0 : n0 + w])
 
         g_codes = keep.tile([P, M], U32, align_bytes=256, name="g_codes")
         g_scales = keep.tile([P, M], U8, align_bytes=256, name="g_scales")
@@ -65,17 +66,16 @@ def tile_mix_ghost_none_kernel(tc, x, xt, g, gt, out):
         xt_codes = keep.tile([P, PASSES, N], U32, align_bytes=256, name="xt_codes")
         xt_scales = keep.tile([P, PASSES, N], U8, align_bytes=256, name="xt_scales")
         u = keep.tile([P, M_TILES, N], F32, name="u")
-        res = [keep.tile([P, M_TILES, w], F32, name="res%d" % q) for q, (n0, w) in enumerate(CHUNKS)]
+        res = keep.tile([P, M_TILES, N], F32, name="res")
 
-        def interleave(raw, width, share):
+        def round_block(raw, width, split):
             grouped = group_pool.tile([P, BLOCK, PACK], BF16, align_bytes=256, name="grouped")
-            for copy, lo, hi in ((nc.vector.tensor_copy, 0, share), (nc.scalar.copy, share, width)):
-                if lo == hi:
-                    continue
-                copy(
-                    out=grouped[:, lo:hi, :].rearrange("p (c i) t -> p c t i", i=4),
-                    in_=raw[:, :, lo:hi].rearrange("p t (c i) -> p c t i", i=4),
-                )
+            for copy, lo, hi in ((nc.vector.tensor_copy, 0, split), (nc.scalar.copy, split, width)):
+                if lo < hi:
+                    copy(
+                        out=grouped[:, lo:hi, :].rearrange("p (c i) t -> p c t i", i=4),
+                        in_=raw[:, :, lo:hi].rearrange("p t (c i) -> p c t i", i=4),
+                    )
             return grouped
 
         def quantize(grouped, width, codes, scales, fmt):
@@ -85,107 +85,103 @@ def tile_mix_ghost_none_kernel(tc, x, xt, g, gt, out):
                 in_=grouped[:, :width, :].rearrange("p w j -> p (w j)"),
             )
 
-        def run(blocks):
-            pending = None
-            for raw, width, share, codes, scales, fmt, then in blocks:
-                grouped = interleave(raw, width, share)
-                if pending is not None:
-                    pending()
-                def finish(grouped=grouped, width=width, codes=codes, scales=scales, fmt=fmt, then=then):
-                    quantize(grouped, width, codes, scales, fmt)
-                    then()
-                pending = finish
-            pending()
-
-        def nothing():
-            return None
-
-        def u_block(b):
-            cols = slice(b * BLOCK, (b + 1) * BLOCK)
+        def product(banks, lhs, rhs, fmt, start, stop):
+            (lhs_codes, lhs_scales), (rhs_codes, rhs_scales) = lhs, rhs
             for m in range(M_TILES):
                 mc = slice(m * P, (m + 1) * P)
-                bank = psum.tile([P, BLOCK], F32, name="bank")
                 nc.tensor.matmul_mx(
-                    out=bank[:],
-                    lhsT=g_codes[:, mc].bitcast(E5M2X4),
-                    lhsT_scale=g_scales[:, mc],
-                    rhs=gt_codes[:, cols].bitcast(E5M2X4),
-                    rhs_scale=gt_scales[:, cols],
-                    start=True,
-                    stop=True,
+                    out=banks[m],
+                    lhsT=lhs_codes[:, mc].bitcast(fmt),
+                    lhsT_scale=lhs_scales[:, mc],
+                    rhs=rhs_codes.bitcast(fmt),
+                    rhs_scale=rhs_scales,
+                    start=start,
+                    stop=stop,
                 )
-                nc.scalar.copy(out=u[:, m, cols], in_=bank[:])
 
-        blocks = [(g_raw[:], M, 160, g_codes[:], g_scales[:], E5M2X4, nothing)]
-        for b in range(N // BLOCK):
-            cols = slice(b * BLOCK, (b + 1) * BLOCK)
-            blocks.append((gt_raw[:, :, cols], BLOCK, 256, gt_codes[:, cols], gt_scales[:, cols], E5M2X4, partial(u_block, b)))
-        run(blocks)
-
-        def x_blocks(cs):
-            return [(x_raw[c][:], M, 128, x_codes[:, c, :], x_scales[:, c, :], E4M3X4, nothing) for c in cs]
-
-        run(x_blocks(range(EARLY_X)))
+        def u_block(cols):
+            banks = [psum.tile([P, BLOCK], F32, name="bank") for m in range(M_TILES)]
+            product([bank[:] for bank in banks], (g_codes[:], g_scales[:]), (gt_codes[:, cols], gt_scales[:, cols]), E5M2X4, True, True)
+            for m in range(M_TILES):
+                nc.scalar.copy(out=u[:, m, cols], in_=banks[m][:])
 
         acc = []
-        for q in range(len(CHUNKS)):
-            acc.append([psum.tile([P, BLOCK], F32, name="bank") for m in range(M_TILES)])
 
         def a_chunk(c, q):
-            n0, w = CHUNKS[q]
+            n0, w, v = CHUNKS[q]
             cols = slice(n0, n0 + w)
-            for m in range(M_TILES):
-                mc = slice(m * P, (m + 1) * P)
-                nc.tensor.matmul_mx(
-                    out=acc[q][m][:, :w],
-                    lhsT=x_codes[:, c, mc].bitcast(E4M3X4),
-                    lhsT_scale=x_scales[:, c, mc],
-                    rhs=xt_codes[:, c, cols].bitcast(E4M3X4),
-                    rhs_scale=xt_scales[:, c, cols],
-                    start=(c == 0),
-                    stop=(c == PASSES - 1),
-                )
+            if c == 0:
+                acc.append([psum.tile([P, BLOCK], F32, name="bank") for m in range(M_TILES)])
+            product(
+                [bank[:, :w] for bank in acc[q]],
+                (x_codes[:, c, :], x_scales[:, c, :]),
+                (xt_codes[:, c, cols], xt_scales[:, c, cols]),
+                E4M3X4,
+                c == 0,
+                c == LAST,
+            )
 
         def a_chunks(c, qs):
             for q in qs:
                 a_chunk(c, q)
 
-        for c in range(PASSES - 1):
-            blocks = []
+        def nothing():
+            return None
+
+        def multiply(q, m):
+            n0, w, v = CHUNKS[q]
+            cols = slice(n0, n0 + w)
+            nc.vector.tensor_tensor(out=res[:, m, cols], in0=acc[q][m][:, :w], in1=u[:, m, cols], op=MULT)
+            nc.sync.dma_start(out=out[m * P : (m + 1) * P, cols], in_=res[:, m, cols])
+
+        def x_block(c):
+            return (x_raw[c], M, 128, x_codes[:, c, :], x_scales[:, c, :], E4M3X4, nothing)
+
+        def xt_blocks(c):
+            found = []
             for b, qs in enumerate(((0,), (1,), (2, 3))):
                 cols = slice(b * BLOCK, (b + 1) * BLOCK)
-                then = partial(a_chunks, c, qs) if c < EARLY_X else nothing
-                blocks.append((xt_raw[c][:, :, cols], BLOCK, 288, xt_codes[:, c, cols], xt_scales[:, c, cols], E4M3X4, then))
-            run(blocks)
-        run(x_blocks(range(EARLY_X, PASSES)))
-        for c in range(EARLY_X, PASSES - 1):
-            a_chunks(c, range(len(CHUNKS)))
+                found.append((xt_raw[c][:, :, cols], BLOCK, 288, xt_codes[:, c, cols], xt_scales[:, c, cols], E4M3X4, partial(a_chunks, c, qs)))
+            return found
 
-        last = PASSES - 1
-        grouped_of = {}
-
-        def copy(q):
-            grouped_of[q] = interleave(last_raw[q][:], CHUNKS[q][1], LAST_SHARE[q])
-
-        def quant(q):
-            n0, w = CHUNKS[q]
+        def chunk_block(q):
+            n0, w, v = CHUNKS[q]
             cols = slice(n0, n0 + w)
-            quantize(grouped_of[q], w, xt_codes[:, last, cols], xt_scales[:, last, cols], E4M3X4)
-            a_chunk(last, q)
+            return (chunk_raw[q][:], w, v, xt_codes[:, LAST, cols], xt_scales[:, LAST, cols], E4M3X4, partial(a_chunk, LAST, q))
 
-        def mul(q, m):
-            n0, w = CHUNKS[q]
-            nc.vector.tensor_tensor(out=res[q][:, m, :], in0=acc[q][m][:, :w], in1=u[:, m, n0 : n0 + w], op=MULT)
-            nc.sync.dma_start(out=out[m * P : (m + 1) * P, n0 : n0 + w], in_=res[q][:, m, :])
+        def begin(block):
+            raw, width, split = block[:3]
+            return (round_block(raw, width, split), block)
 
-        copy(0)
-        quant(0)
-        copy(1)
-        mul(0, 0)
+        def end(begun):
+            grouped, (raw, width, split, codes, scales, fmt, use) = begun
+            quantize(grouped, width, codes, scales, fmt)
+            use()
+
+        def run(blocks):
+            begun = begin(blocks[0])
+            for block in blocks[1:]:
+                following = begin(block)
+                end(begun)
+                begun = following
+            return begun
+
+        first = [(g_raw[:], M, 128, g_codes[:], g_scales[:], E5M2X4, nothing)]
+        for b in range(N // BLOCK):
+            cols = slice(b * BLOCK, (b + 1) * BLOCK)
+            first.append((gt_raw[:, :, cols], BLOCK, 256, gt_codes[:, cols], gt_scales[:, cols], E5M2X4, partial(u_block, cols)))
+        end(run(first))
+        end(run([x_block(c) for c in range(LAST)]))
+        for c in range(LAST - 1):
+            end(run(xt_blocks(c)))
+        begun = run(xt_blocks(LAST - 1) + [x_block(LAST), chunk_block(0)])
+        end(begun)
+        begun = begin(chunk_block(1))
+        multiply(0, 0)
         for q in range(1, len(CHUNKS)):
-            quant(q)
+            end(begun)
             if q + 1 < len(CHUNKS):
-                copy(q + 1)
-            mul(q - 1, 1)
-            mul(q, 0)
-        mul(len(CHUNKS) - 1, 1)
+                begun = begin(chunk_block(q + 1))
+            multiply(q - 1, 1)
+            multiply(q, 0)
+        multiply(len(CHUNKS) - 1, 1)

from contextlib import ExitStack
from functools import partial

import concourse.mybir as mybir

K, L, M, N = 2048, 512, 256, 1536
FLOPS = 2 * M * N * (K + L)

F32 = mybir.dt.float32
BF16 = mybir.dt.bfloat16
U32 = mybir.dt.uint32
U8 = mybir.dt.uint8
E4M3X4 = mybir.dt.float8_e4m3fn_x4
E5M2X4 = mybir.dt.float8_e5m2_x4
MULT = mybir.AluOpType.mult

P = 128
PACK = 4
K_PASS = P * PACK
PASSES = K // K_PASS
LAST = PASSES - 1
BLOCK = 512
M_TILES = M // P

CHUNKS = [(0, 512, 256), (512, 512, 288), (1024, 256, 0), (1280, 256, 0)]


def tile_mix_ghost_none_kernel(tc, x, xt, g, gt, out):
    nc = tc.nc
    with ExitStack() as ctx:
        ctx.enter_context(tc.manual_schedule())
        raws = ctx.enter_context(tc.tile_pool(name="raws", bufs=1))
        keep = ctx.enter_context(tc.tile_pool(name="keep", bufs=1))
        group_pool = ctx.enter_context(tc.tile_pool(name="groups", bufs=4))
        psum = ctx.enter_context(tc.psum_pool(name="psum", bufs=8))

        def rows(ap, c):
            return ap[c * K_PASS : (c + 1) * K_PASS, :].rearrange("(p j) n -> p j n", j=PACK)

        g_raw = raws.tile([P, PACK, M], F32, name="g_raw")
        gt_raw = raws.tile([P, PACK, N], F32, name="gt_raw")
        x_early = raws.tile([P, LAST, PACK, M], F32, name="x_early")
        x_last = raws.tile([P, PACK, M], F32, name="x_last")
        xt_raw = [raws.tile([P, PACK, N], F32, name="xt_raw%d" % c) for c in range(LAST)]
        chunk_raw = [raws.tile([P, PACK, w], F32, name="chunk_raw%d" % q) for q, (n0, w, v) in enumerate(CHUNKS)]
        x_raw = [x_early[:, c] for c in range(LAST)] + [x_last[:]]

        nc.sync.dma_start(out=g_raw[:], in_=rows(g, 0))
        nc.sync.dma_start(out=gt_raw[:], in_=rows(gt, 0))
        nc.sync.dma_start(
            out=x_early[:].rearrange("p c j m -> p c (j m)"),
            in_=x[: LAST * K_PASS, :].rearrange("(c p j) m -> p c (j m)", p=P, j=PACK),
        )
        for c in range(LAST):
            nc.sync.dma_start(out=xt_raw[c][:], in_=rows(xt, c))
        nc.sync.dma_start(out=x_last[:], in_=rows(x, LAST))
        for q, (n0, w, v) in enumerate(CHUNKS):
            nc.sync.dma_start(out=chunk_raw[q][:], in_=rows(xt, LAST)[:, :, n0 : n0 + w])

        g_codes = keep.tile([P, M], U32, align_bytes=256, name="g_codes")
        g_scales = keep.tile([P, M], U8, align_bytes=256, name="g_scales")
        gt_codes = keep.tile([P, N], U32, align_bytes=256, name="gt_codes")
        gt_scales = keep.tile([P, N], U8, align_bytes=256, name="gt_scales")
        x_codes = keep.tile([P, PASSES, M], U32, align_bytes=256, name="x_codes")
        x_scales = keep.tile([P, PASSES, M], U8, align_bytes=256, name="x_scales")
        xt_codes = keep.tile([P, PASSES, N], U32, align_bytes=256, name="xt_codes")
        xt_scales = keep.tile([P, PASSES, N], U8, align_bytes=256, name="xt_scales")
        u = keep.tile([P, M_TILES, N], F32, name="u")
        res = keep.tile([P, M_TILES, N], F32, name="res")

        def round_block(raw, width, split):
            grouped = group_pool.tile([P, BLOCK, PACK], BF16, align_bytes=256, name="grouped")
            for copy, lo, hi in ((nc.vector.tensor_copy, 0, split), (nc.scalar.copy, split, width)):
                if lo < hi:
                    copy(
                        out=grouped[:, lo:hi, :].rearrange("p (c i) t -> p c t i", i=4),
                        in_=raw[:, :, lo:hi].rearrange("p t (c i) -> p c t i", i=4),
                    )
            return grouped

        def quantize(grouped, width, codes, scales, fmt):
            nc.vector.quantize_mx(
                out=codes.bitcast(fmt),
                scales=scales,
                in_=grouped[:, :width, :].rearrange("p w j -> p (w j)"),
            )

        def product(banks, lhs, rhs, fmt, start, stop):
            (lhs_codes, lhs_scales), (rhs_codes, rhs_scales) = lhs, rhs
            for m in range(M_TILES):
                mc = slice(m * P, (m + 1) * P)
                nc.tensor.matmul_mx(
                    out=banks[m],
                    lhsT=lhs_codes[:, mc].bitcast(fmt),
                    lhsT_scale=lhs_scales[:, mc],
                    rhs=rhs_codes.bitcast(fmt),
                    rhs_scale=rhs_scales,
                    start=start,
                    stop=stop,
                )

        def u_block(cols):
            banks = [psum.tile([P, BLOCK], F32, name="bank") for m in range(M_TILES)]
            product([bank[:] for bank in banks], (g_codes[:], g_scales[:]), (gt_codes[:, cols], gt_scales[:, cols]), E5M2X4, True, True)
            for m in range(M_TILES):
                nc.scalar.copy(out=u[:, m, cols], in_=banks[m][:])

        acc = []

        def a_chunk(c, q):
            n0, w, v = CHUNKS[q]
            cols = slice(n0, n0 + w)
            if c == 0:
                acc.append([psum.tile([P, BLOCK], F32, name="bank") for m in range(M_TILES)])
            product(
                [bank[:, :w] for bank in acc[q]],
                (x_codes[:, c, :], x_scales[:, c, :]),
                (xt_codes[:, c, cols], xt_scales[:, c, cols]),
                E4M3X4,
                c == 0,
                c == LAST,
            )

        def a_chunks(c, qs):
            for q in qs:
                a_chunk(c, q)

        def nothing():
            return None

        def multiply(q, m):
            n0, w, v = CHUNKS[q]
            cols = slice(n0, n0 + w)
            nc.vector.tensor_tensor(out=res[:, m, cols], in0=acc[q][m][:, :w], in1=u[:, m, cols], op=MULT)
            nc.sync.dma_start(out=out[m * P : (m + 1) * P, cols], in_=res[:, m, cols])

        def x_block(c):
            return (x_raw[c], M, 128, x_codes[:, c, :], x_scales[:, c, :], E4M3X4, nothing)

        def xt_blocks(c):
            found = []
            for b, qs in enumerate(((0,), (1,), (2, 3))):
                cols = slice(b * BLOCK, (b + 1) * BLOCK)
                found.append((xt_raw[c][:, :, cols], BLOCK, 288, xt_codes[:, c, cols], xt_scales[:, c, cols], E4M3X4, partial(a_chunks, c, qs)))
            return found

        def chunk_block(q):
            n0, w, v = CHUNKS[q]
            cols = slice(n0, n0 + w)
            return (chunk_raw[q][:], w, v, xt_codes[:, LAST, cols], xt_scales[:, LAST, cols], E4M3X4, partial(a_chunk, LAST, q))

        def begin(block):
            raw, width, split = block[:3]
            return (round_block(raw, width, split), block)

        def end(begun):
            grouped, (raw, width, split, codes, scales, fmt, use) = begun
            quantize(grouped, width, codes, scales, fmt)
            use()

        def run(blocks):
            begun = begin(blocks[0])
            for block in blocks[1:]:
                following = begin(block)
                end(begun)
                begun = following
            return begun

        first = [(g_raw[:], M, 128, g_codes[:], g_scales[:], E5M2X4, nothing)]
        for b in range(N // BLOCK):
            cols = slice(b * BLOCK, (b + 1) * BLOCK)
            first.append((gt_raw[:, :, cols], BLOCK, 256, gt_codes[:, cols], gt_scales[:, cols], E5M2X4, partial(u_block, cols)))
        end(run(first))
        end(run([x_block(c) for c in range(LAST)]))
        for c in range(LAST - 1):
            end(run(xt_blocks(c)))
        begun = run(xt_blocks(LAST - 1) + [x_block(LAST), chunk_block(0)])
        end(begun)
        begun = begin(chunk_block(1))
        multiply(0, 0)
        for q in range(1, len(CHUNKS)):
            end(begun)
            if q + 1 < len(CHUNKS):
                begun = begin(chunk_block(q + 1))
            multiply(q - 1, 1)
            multiply(q, 0)
        multiply(len(CHUNKS) - 1, 1)
